import numpy as np
import ml_dtypes


def mxq(x, axis, fmt="e4m3"):
    dtype, down = {"e4m3": (ml_dtypes.float8_e4m3fn, 7), "e5m2": (ml_dtypes.float8_e5m2, 14)}[fmt]
    v = np.moveaxis(np.asarray(x, np.float32).astype(ml_dtypes.bfloat16).astype(np.float64), axis, -1)
    blocks = v.reshape(v.shape[:-1] + (-1, 32))
    amax = np.abs(blocks).max(-1, keepdims=True)
    byte = np.maximum(np.where(amax > 0, np.frexp(amax)[1] - 1 + 127, 0) - down, 1)
    scale = np.exp2(byte - 127.0)
    codes = (blocks / scale).astype(np.float32).astype(dtype).astype(np.float64)
    return np.moveaxis((codes * scale).reshape(v.shape), -1, axis)


WIDE = False


def mx_kscale(k):
    if not WIDE:
        return np.ones(k)
    levels = np.array([10, -10, 5, -5, 0])
    if k % 512:
        return np.exp2(np.random.permutation(np.resize(levels, k // 32))).repeat(32)
    a = np.empty((k // 512, 16))
    for p in range(k // 512):
        a[p, :8] = np.random.permutation(np.resize(levels, 8))
        for g in range(8):
            far = levels[np.abs(levels - a[p, g]) >= 10]
            a[p, g + 8] = far[np.random.randint(len(far))]
    return np.exp2(a.ravel()).repeat(32)


BF16 = ml_dtypes.bfloat16


def bf(x):
    return np.asarray(x, np.float32).astype(BF16)


def f64(x):
    return np.asarray(x).astype(np.float64)

def planes(Y):
    n, m = Y.shape
    b = f64(bf(Y)).reshape(n // 32, 32, m)
    amax = np.abs(b).max(1)
    byte = np.clip(np.where(amax > 0, np.frexp(amax)[1] - 1 + 127 - 7, 1), 1, 254)
    codes = (b * np.exp2(127.0 - byte)[:, None, :]).reshape(n, m).astype(np.float32).astype(ml_dtypes.float8_e4m3fn).view(np.uint8)
    words = codes.reshape(n // 512, 128, 4, m).transpose(0, 1, 3, 2)
    return np.ascontiguousarray(words), np.ascontiguousarray(byte.astype(np.uint8).reshape(n // 512, 16, m))


R, L, C, G = 1536, 512, 1024, 2048


def setup_inputs():
    s = mx_kscale(L)
    t = mx_kscale(R)
    affinity = np.exp(1.2 * np.random.randn(R, L) + 0.5 * np.random.randn(R, 1)) / (4.0 * L)
    doses = np.exp(1.2 * np.random.randn(L, C) + 0.7 * np.random.randn(1, C))
    density = np.exp(0.3 * np.random.randn(R))
    signalling = 3.0 * np.random.randn(R, G) / np.sqrt(R)
    return {
        "affinity": bf(affinity * s[None, :]),
        "doses": bf(doses / s[:, None]),
        "density": bf(density * t),
        "signalling": bf(signalling / t[:, None]),
        "basal": bf(0.4 * np.random.randn(G)),
        "vmax": bf(np.exp(0.8 * np.random.randn(G))),
        "access": bf(np.exp(0.5 * np.random.randn(G, C))),
    }


def reference(affinity, doses, density, signalling, basal, vmax, access):
    u = mxq(f64(affinity), 1, "e4m3") @ mxq(f64(doses), 0, "e4m3")
    h = u / (1.0 + u) * f64(density)[:, None]
    z = mxq(f64(signalling), 0, "e4m3").T @ mxq(h, 0, "e4m3")
    act = 1.0 / (1.0 + np.exp(-(z + f64(basal)[:, None])))
    y = act * f64(vmax)[:, None] * f64(access)
    Y = y
    words, scales = planes(Y)
    return y, words, scales

@@ -1,0 +1,397 @@
+from contextlib import ExitStack
+
+import concourse.mybir as mybir
+from concourse.masks import make_identity
+
+R, L, C, G = 1536, 512, 1024, 2048
+FLOPS = 2 * R * L * C + 2 * R * G * C
+
+F32 = mybir.dt.float32
+BF16 = mybir.dt.bfloat16
+U32 = mybir.dt.uint32
+I32 = mybir.dt.int32
+U8 = mybir.dt.uint8
+FP8X4 = mybir.dt.float8_e4m3fn_x4
+ACT = mybir.ActivationFunctionType
+MULT = mybir.AluOpType.mult
+
+P = 128
+PACK = 4
+GROUP = P * PACK
+HALF = 512
+RQ = R // GROUP
+GQ = G // GROUP
+CH = C // HALF
+VEC_ROWS = 12
+LATE = (3,)
+TINY = 2.0 ** -60
+
+
+def tile_receptor_occupancy_transcription_h3_kernel(
+    tc, affinity, doses, density, signalling, basal, vmax, access, out_0, out_1, out_2
+):
+    nc = tc.nc
+    with ExitStack() as ctx:
+        keep = ctx.enter_context(tc.tile_pool(name="keep", bufs=1))
+        small = ctx.enter_context(tc.tile_pool(name="small", bufs=8))
+        large = ctx.enter_context(tc.tile_pool(name="large", bufs=9))
+        wide = ctx.enter_context(tc.tile_pool(name="wide", bufs=7))
+        ywords = ctx.enter_context(tc.tile_pool(name="ywords", bufs=3))
+        psum = ctx.enter_context(tc.psum_pool(name="psum", bufs=8))
+        ctx.enter_context(tc.manual_schedule())
+
+        t_ = {}
+
+        def staged(key):
+            t_[key] = small.tile([P, GROUP * PACK], BF16, name="staged", tag="small", align_bytes=64)
+            return t_[key]
+
+        def operand(key, width):
+            name = "_".join(str(k) for k in key)
+            codes = keep.tile([P, width], U32, name="codes_" + name, align_bytes=64)
+            scales = keep.tile([P, width], U8, name="scales_" + name, align_bytes=64)
+            t_[key] = (codes, scales)
+            return t_[key]
+
+        def quantise(src_key, dst_key):
+            codes, scales = operand(dst_key, GROUP)
+            nc.vector.quantize_mx(out=codes[:].bitcast(FP8X4), scales=scales[:], in_=t_[src_key][:])
+
+        ident = keep.tile([P, P], F32, name="ident")
+        tiny = keep.tile([P, 1], F32, name="tiny")
+        warm = keep.tile([P, 1], F32, name="warm")
+        rows = keep.tile([P, GROUP], BF16, name="rows")
+        vecs = keep.tile([P, VEC_ROWS, PACK], BF16, name="vecs")
+        dens = vecs[:, 0:RQ, :]
+        bas = vecs[:, 4 : 4 + GQ, :]
+        vm = vecs[:, 8 : 8 + GQ, :]
+        nc.gpsimd.memset(tiny[:], TINY)
+        make_identity(nc, ident[:])
+        nc.gpsimd.memset(rows[:].bitcast(I32), 0)
+        nc.scalar.activation(out=warm[:], in_=tiny[:], func=ACT.Ln, bias=tiny[:])
+
+        def load_aff(q):
+            raw = staged(("aff_raw", q))
+            nc.sync.dma_start(
+                out=raw[:].rearrange("p (t k) -> p t k", t=PACK),
+                in_=affinity[q * GROUP : (q + 1) * GROUP, :].rearrange("(m t) k -> m t k", t=PACK),
+            )
+
+        def load_doses(c):
+            raw = staged(("dos_raw", c))
+            nc.sync.dma_start(
+                out=raw[:].rearrange("p (j w) -> p j w", j=PACK),
+                in_=doses[:, c * HALF : (c + 1) * HALF].rearrange("(p j) w -> p j w", j=PACK),
+            )
+
+        def load_sig(q, gg):
+            raw = large.tile([P, PACK, 2 * GROUP], BF16, name="sig_raw", tag="large")
+            t_["sig_raw", q, gg] = raw
+            nc.sync.dma_start(
+                out=raw[:],
+                in_=signalling[q * GROUP : (q + 1) * GROUP, gg * 2 * GROUP : (gg + 1) * 2 * GROUP].rearrange(
+                    "(p j) w -> p j w", j=PACK
+                ),
+            )
+
+        def load_access(g):
+            raw = large.tile([P, PACK, C], BF16, name="acc_raw", tag="large")
+            t_["access", g] = raw
+            nc.sync.dma_start(
+                out=raw[:], in_=access[g * GROUP : (g + 1) * GROUP, :].rearrange("(p t) w -> p t w", t=PACK)
+            )
+
+        def load_vecs():
+            for first, vec, q0, q1 in [(0, density, 0, 2), (2, density, 2, 3), (4, basal, 0, GQ), (8, vmax, 0, GQ)]:
+                nc.sync.dma_start(
+                    out=rows[first : first + q1 - q0, :], in_=vec.rearrange("(q k) -> q k", k=GROUP)[q0:q1, :]
+                )
+
+        def turn_vecs():
+            words = rows[:].bitcast(F32)
+            bank = psum.tile([P, 2, P], F32, name="bank", tag="bank")
+            for u in range(2):
+                nc.tensor.transpose(bank[:, u, :], words[:, u : GROUP // 2 : 2], ident[:])
+            t_["vec_bank"] = bank
+
+        def empty_vecs():
+            bank = t_["vec_bank"]
+            nc.vector.tensor_copy(
+                out=vecs[:].rearrange("p r t -> p (r t)").bitcast(F32).rearrange("p (r u) -> p r u", u=2),
+                in_=bank[:, :, 0:VEC_ROWS].rearrange("p u r -> p r u"),
+            )
+
+        def turn_aff(q, pair):
+            words = t_["aff_raw", q][:].bitcast(F32).rearrange("p (t w) -> p t w", t=PACK)
+            bank = psum.tile([P, 2, 2, P], F32, name="bank", tag="bank")
+            t_["aff_bank", q, pair] = bank
+            for tt in range(2):
+                for u in range(2):
+                    nc.tensor.transpose(bank[:, tt, u, :], words[:, 2 * pair + tt, u : L // 2 : 2], ident[:])
+
+        def empty_aff(q, pair):
+            if pair == 0:
+                staged(("aff_in", q))
+            dst = t_["aff_in", q][:].bitcast(F32).rearrange("p (t m u) -> p t m u", t=PACK, u=2)
+            nc.scalar.copy(
+                out=dst[:, 2 * pair : 2 * pair + 2, :, :],
+                in_=t_["aff_bank", q, pair][:].rearrange("p t u m -> p t m u"),
+            )
+
+        def weave_doses(c):
+            dst = staged(("dos_in", c))
+            nc.vector.tensor_copy(
+                out=dst[:].rearrange("p (w i j) -> p w j i", i=4, j=PACK),
+                in_=t_["dos_raw", c][:].rearrange("p (j w i) -> p w j i", j=PACK, i=4),
+            )
+
+        def drive(q, c, b):
+            bank = psum.tile([P, PACK, P], F32, name="bank", tag="bank")
+            a_codes, a_scales = t_["aff", q]
+            d_codes, d_scales = t_["dos", c]
+            wells = slice(b * P, (b + 1) * P)
+            for t in range(PACK):
+                cols = slice(t * P, (t + 1) * P)
+                nc.tensor.matmul_mx(
+                    out=bank[:, t, :],
+                    lhsT=a_codes[:, cols].bitcast(FP8X4),
+                    lhsT_scale=a_scales[:, cols],
+                    rhs=d_codes[:, wells].bitcast(FP8X4),
+                    rhs_scale=d_scales[:, wells],
+                    start=True,
+                    stop=True,
+                )
+            if b == 0:
+                t_["bound", q, c] = wide.tile([P, HALF, PACK], F32, name="bound", tag="wide")
+            nc.scalar.activation(
+                out=t_["bound", q, c][:, wells, :], in_=bank[:].rearrange("p t w -> p w t"), func=ACT.Ln, bias=tiny[:]
+            )
+
+        def saturate(q, c):
+            bound = t_["bound", q, c]
+            nc.scalar.activation(out=bound[:], in_=bound[:], func=ACT.Sigmoid)
+
+        def occupy(q, c):
+            dst = staged(("h_in", q, c))
+            nc.vector.tensor_tensor(
+                out=dst[:].rearrange("p (w t) -> p w t", t=PACK),
+                in0=t_["bound", q, c][:],
+                in1=dens[:, q, :].unsqueeze(1).to_broadcast([P, HALF, PACK]),
+                op=MULT,
+            )
+
+        def weave_sig(q, g, on_scalar=False):
+            dst = staged(("sig_in", q, g))
+            raw = t_["sig_raw", q, g // 2][:, :, (g % 2) * GROUP : (g % 2 + 1) * GROUP]
+            copy = nc.scalar.copy if on_scalar else nc.vector.tensor_copy
+            copy(
+                out=dst[:].rearrange("p (t m j) -> p m j t", t=PACK, j=PACK),
+                in_=raw.rearrange("p j (m t) -> p m j t", t=PACK),
+            )
+
+        def signal_pass(g, c, t, q):
+            if q == 0:
+                t_["z", g, c, t] = psum.tile([P, HALF], F32, name="bank", tag="bank")
+            s_codes, s_scales = t_["sig", q, g]
+            h_codes, h_scales = t_["h", q, c]
+            cols = slice(t * P, (t + 1) * P)
+            nc.tensor.matmul_mx(
+                out=t_["z", g, c, t][:],
+                lhsT=s_codes[:, cols].bitcast(FP8X4),
+                lhsT_scale=s_scales[:, cols],
+                rhs=h_codes[:].bitcast(FP8X4),
+                rhs_scale=h_scales[:],
+                start=(q == 0),
+                stop=(q == RQ - 1),
+            )
+
+        def activate(g, c, t):
+            if t == 0:
+                t_["y", g, c] = wide.tile([P, PACK, HALF], F32, name="y", tag="wide")
+            nc.scalar.activation(
+                out=t_["y", g, c][:, t, :], in_=t_["z", g, c, t][:], func=ACT.Sigmoid, bias=bas[:, g, t : t + 1]
+            )
+
+        def transcribe(g, c, t):
+            y = t_["y", g, c][:, t, :]
+            nc.vector.scalar_tensor_tensor(
+                out=y,
+                in0=y,
+                scalar=vm[:, g, t : t + 1],
+                in1=t_["access", g][:, t, c * HALF : (c + 1) * HALF],
+                op0=MULT,
+                op1=MULT,
+            )
+
+        def store_y(g, c, t0, t1):
+            rows = out_0[g * GROUP : (g + 1) * GROUP, c * HALF : (c + 1) * HALF].rearrange("(p t) w -> p t w", t=PACK)
+            nc.sync.dma_start(out=rows[:, t0:t1, :], in_=t_["y", g, c][:, t0:t1, :])
+
+        def round_y(g, c, part, on_scalar):
+            if part == 0:
+                staged(("y_in", g, c))
+            half = HALF // 2
+            dst = t_["y_in", g, c][:, part * half * PACK : (part + 1) * half * PACK]
+            src = t_["y", g, c][:, :, part * half : (part + 1) * half]
+            dst = dst.rearrange("p (w i t) -> p w t i", i=4, t=PACK)
+            src = src.rearrange("p t (w i) -> p w t i", i=4)
+            if on_scalar:
+                nc.scalar.copy(out=dst, in_=src)
+            else:
+                nc.vector.tensor_copy(out=dst, in_=src)
+
+        def quantise_y(g, c, w0, w1):
+            if w0 == 0:
+                t_["y_codes", g, c] = ywords.tile([P, HALF], U32, name="y_codes", tag="ywords", align_bytes=64)
+            if w0 == 0 and c == 0:
+                t_["y_scales", g] = keep.tile([P, C], U8, name="y_scales_%d" % g, align_bytes=64)
+            codes = t_["y_codes", g, c][:, w0:w1]
+            nc.vector.quantize_mx(
+                out=codes.bitcast(FP8X4),
+                scales=t_["y_scales", g][:, c * HALF + w0 : c * HALF + w1],
+                in_=t_["y_in", g, c][:, w0 * PACK : w1 * PACK],
+            )
+            words = out_1[g].rearrange("p w t -> p (w t)").bitcast(I32)
+            nc.sync.dma_start(out=words[:, c * HALF + w0 : c * HALF + w1], in_=codes.bitcast(I32))
+
+        def store_scales(g):
+            for quad in range(4):
+                nc.sync.dma_start(
+                    out=out_2[g, 4 * quad : 4 * quad + 4, :].bitcast(I32),
+                    in_=t_["y_scales", g][32 * quad : 32 * quad + 4, :].bitcast(I32),
+                )
+
+
+        load_aff(0)
+        load_doses(0)
+        load_aff(1)
+        load_aff(2)
+        load_sig(0, 0)
+        load_doses(1)
+        load_sig(1, 0)
+        load_sig(2, 0)
+        load_vecs()
+        for q in range(RQ):
+            load_sig(q, 1)
+        for g in range(GQ - 1):
+            load_access(g)
+
+        for pair in range(2):
+            turn_aff(0, pair)
+            empty_aff(0, pair)
+        weave_doses(0)
+        for pair in range(2):
+            turn_aff(1, pair)
+            empty_aff(1, pair)
+        quantise(("aff_in", 0), ("aff", 0))
+        quantise(("dos_in", 0), ("dos", 0))
+        def quantise_sig(q, g):
+            quantise(("sig_in", q, g), ("sig", q, g))
+
+        def quantise_h(q, c):
+            quantise(("h_in", q, c), ("h", q, c))
+
+        drive(0, 0, 0)
+        drive(0, 0, 1)
+        quantise(("aff_in", 1), ("aff", 1))
+        for pair in range(2):
+            turn_aff(2, pair)
+            empty_aff(2, pair)
+        drive(0, 0, 2)
+        drive(0, 0, 3)
+        weave_sig(0, 0)
+        quantise(("aff_in", 2), ("aff", 2))
+        weave_doses(1)
+        quantise_sig(0, 0)
+        weave_sig(0, 1)
+        quantise(("dos_in", 1), ("dos", 1))
+        for q, c in [(1, 0), (2, 0), (0, 1), (1, 1), (2, 1)]:
+            for b in range(4):
+                drive(q, c, b)
+        turn_vecs()
+
+        sig_steps = [(0, 1), (1, 0), (1, 1), (2, 0), (2, 1), (0, 2)]
+        for i in range(1, len(sig_steps) + 1):
+            if i < len(sig_steps):
+                weave_sig(*sig_steps[i])
+            else:
+                empty_vecs()
+            quantise_sig(*sig_steps[i - 1])
+        load_access(GQ - 1)
+
+        tiles = [(0, 0), (1, 0), (2, 0), (0, 1), (1, 1), (2, 1), (3, 0), (3, 1)]
+        for c in range(CH):
+            for q in range(RQ):
+                saturate(q, c)
+        occupy(0, 0)
+        occupy(1, 0)
+        quantise_h(0, 0)
+        occupy(2, 0)
+        quantise_h(1, 0)
+        weave_sig(1, 2)
+        quantise_h(2, 0)
+        weave_sig(2, 2)
+        quantise_sig(1, 2)
+        occupy(0, 1)
+        quantise_sig(2, 2)
+        for q in range(RQ):
+            for t in range(PACK):
+                signal_pass(0, 0, t, q)
+        for t in range(PACK):
+            for q in range(RQ):
+                signal_pass(*tiles[1], t, q)
+
+        def cast(i, part, on_scalar):
+            return lambda: round_y(*tiles[i], part, on_scalar)
+
+        def finish(i):
+            def run():
+                quantise_y(*tiles[i], 0, HALF)
+                if tiles[i][1] == CH - 1:
+                    store_scales(tiles[i][0])
+            return run
+
+        def job(fn, *args):
+            return lambda: fn(*args)
+
+        extras = {
+
+            (0, 3): [job(occupy, 1, 1), job(quantise_h, 0, 1)],
+            (1, 3): [job(occupy, 2, 1), job(quantise_h, 1, 1)],
+            (2, 0): [job(quantise_h, 2, 1)],
+            (2, 3): [cast(0, 0, True), cast(0, 1, True), job(weave_sig, 0, 3, True), cast(1, 0, True), cast(1, 1, True), finish(0), job(weave_sig, 1, 3), job(quantise_sig, 0, 3), finish(1)],
+            (3, 1): [cast(2, 0, True)],
+            (3, 3): [cast(2, 1, True), job(weave_sig, 2, 3), job(quantise_sig, 1, 3), finish(2), job(quantise_sig, 2, 3)],
+            (4, 1): [cast(3, 0, True)],
+            (4, 3): [cast(3, 1, True)],
+            (5, 0): [finish(3)],
+            (5, 3): [cast(4, 0, True)],
+            (6, 1): [cast(5, 0, False)],
+            (6, 3): [cast(4, 1, True), cast(5, 1, False), finish(4), finish(5)],
+            (7, 1): [cast(6, 0, False)],
+            (7, 3): [cast(6, 1, True)],
+
+        }
+        n = len(tiles)
+        for i, (g, c) in enumerate(tiles):
+            for t in range(PACK):
+                activate(g, c, t)
+                transcribe(g, c, t)
+                if t % 2 == 1:
+                    store_y(g, c, t - 1, t + 1)
+                for extra in extras.get((i, t), []):
+                    extra()
+                if i + 1 in LATE and t == 0:
+                    for tt in range(PACK):
+                        for q in range(RQ):
+                            signal_pass(*tiles[i + 1], tt, q)
+                if i + 2 < n and i + 2 not in LATE:
+                    for q in range(RQ):
+                        signal_pass(*tiles[i + 2], t, q)
+        g, c = tiles[-1]
+        round_y(g, c, 0, False)
+        round_y(g, c, 1, True)
+        finish(n - 2)()
+        quantise_y(g, c, 0, HALF // 2)
+        quantise_y(g, c, HALF // 2, HALF)
+        store_scales(g)

@@ -14,6 +14,7 @@ U8 = mybir.dt.uint8
 FP8X4 = mybir.dt.float8_e4m3fn_x4
 ACT = mybir.ActivationFunctionType
 MULT = mybir.AluOpType.mult
+ADD = mybir.AluOpType.add
 
 P = 128
 PACK = 4
@@ -23,7 +24,7 @@ RQ = R // GROUP
 GQ = G // GROUP
 CH = C // HALF
 VEC_ROWS = 12
-LATE = (3,)
+TILES = [(0, 0), (1, 0), (2, 0), (3, 0), (0, 1), (1, 1), (2, 1), (3, 1)]
 TINY = 2.0 ** -60
 
 
@@ -33,11 +34,13 @@ def tile_receptor_occupancy_transcription_h3_kernel(
     nc = tc.nc
     with ExitStack() as ctx:
         keep = ctx.enter_context(tc.tile_pool(name="keep", bufs=1))
-        small = ctx.enter_context(tc.tile_pool(name="small", bufs=8))
+        small = ctx.enter_context(tc.tile_pool(name="small", bufs=7))
         large = ctx.enter_context(tc.tile_pool(name="large", bufs=9))
         wide = ctx.enter_context(tc.tile_pool(name="wide", bufs=7))
         ywords = ctx.enter_context(tc.tile_pool(name="ywords", bufs=3))
-        psum = ctx.enter_context(tc.psum_pool(name="psum", bufs=8))
+        psum = ctx.enter_context(tc.psum_pool(name="psum", bufs=7))
+        psum_vecs = ctx.enter_context(tc.psum_pool(name="psum_vecs", bufs=1))
+        relay = ctx.enter_context(tc.tile_pool(name="relay", bufs=1))
         ctx.enter_context(tc.manual_schedule())
 
         t_ = {}
@@ -60,9 +63,9 @@ def tile_receptor_occupancy_transcription_h3_kernel(
         ident = keep.tile([P, P], F32, name="ident")
         tiny = keep.tile([P, 1], F32, name="tiny")
         warm = keep.tile([P, 1], F32, name="warm")
+        y_scales = keep.tile([P, GQ, C], U8, name="y_scales", align_bytes=64)
         rows = keep.tile([P, GROUP], BF16, name="rows")
         vecs = keep.tile([P, VEC_ROWS, PACK], BF16, name="vecs")
-        dens = vecs[:, 0:RQ, :]
         bas = vecs[:, 4 : 4 + GQ, :]
         vm = vecs[:, 8 : 8 + GQ, :]
         nc.gpsimd.memset(tiny[:], TINY)
@@ -70,11 +73,12 @@ def tile_receptor_occupancy_transcription_h3_kernel(
         nc.gpsimd.memset(rows[:].bitcast(I32), 0)
         nc.scalar.activation(out=warm[:], in_=tiny[:], func=ACT.Ln, bias=tiny[:])
 
-        def load_aff(q):
-            raw = staged(("aff_raw", q))
+        def load_aff(q, t0=0, t1=PACK):
+            if t0 == 0:
+                staged(("aff_raw", q))
             nc.sync.dma_start(
-                out=raw[:].rearrange("p (t k) -> p t k", t=PACK),
-                in_=affinity[q * GROUP : (q + 1) * GROUP, :].rearrange("(m t) k -> m t k", t=PACK),
+                out=t_["aff_raw", q][:].rearrange("p (t k) -> p t k", t=PACK)[:, t0:t1, :],
+                in_=affinity[q * GROUP : (q + 1) * GROUP, :].rearrange("(m t) k -> m t k", t=PACK)[:, t0:t1, :],
             )
 
         def load_doses(c):
@@ -109,7 +113,7 @@ def tile_receptor_occupancy_transcription_h3_kernel(
 
         def turn_vecs():
             words = rows[:].bitcast(F32)
-            bank = psum.tile([P, 2, P], F32, name="bank", tag="bank")
+            bank = psum_vecs.tile([P, 2, P], F32, name="vec_bank")
             for u in range(2):
                 nc.tensor.transpose(bank[:, u, :], words[:, u : GROUP // 2 : 2], ident[:])
             t_["vec_bank"] = bank
@@ -130,10 +134,11 @@ def tile_receptor_occupancy_transcription_h3_kernel(
                     nc.tensor.transpose(bank[:, tt, u, :], words[:, 2 * pair + tt, u : L // 2 : 2], ident[:])
 
         def empty_aff(q, pair):
-            if pair == 0:
+            if ("aff_in", q) not in t_:
                 staged(("aff_in", q))
             dst = t_["aff_in", q][:].bitcast(F32).rearrange("p (t m u) -> p t m u", t=PACK, u=2)
-            nc.scalar.copy(
+            copy = nc.vector.tensor_copy if pair == 1 and q < 2 else nc.scalar.copy
+            copy(
                 out=dst[:, 2 * pair : 2 * pair + 2, :, :],
                 in_=t_["aff_bank", q, pair][:].rearrange("p t u m -> p t m u"),
             )
@@ -173,21 +178,32 @@ def tile_receptor_occupancy_transcription_h3_kernel(
 
         def occupy(q, c):
             dst = staged(("h_in", q, c))
+            pairs = t_["vec_bank"][:].rearrange("p u r -> p (u r)").bitcast(BF16)
+            dens = pairs.rearrange("p (u r e) -> p r u e", u=2, e=2)[:, q : q + 1, :, :]
             nc.vector.tensor_tensor(
-                out=dst[:].rearrange("p (w t) -> p w t", t=PACK),
-                in0=t_["bound", q, c][:],
-                in1=dens[:, q, :].unsqueeze(1).to_broadcast([P, HALF, PACK]),
+                out=dst[:].rearrange("p (w u e) -> p w u e", u=2, e=2),
+                in0=t_["bound", q, c][:].rearrange("p w (u e) -> p w u e", u=2),
+                in1=dens.to_broadcast([P, HALF, 2, 2]),
                 op=MULT,
             )
 
-        def weave_sig(q, g, on_scalar=False):
-            dst = staged(("sig_in", q, g))
+        def weave_sig(q, g, engine="vector", slot=None):
+            if slot == 0:
+                t_["relay"] = relay.tile([P, 2, GROUP * PACK], BF16, name="relay", tag="relay", align_bytes=64)
+            if slot is not None:
+                dst = t_["relay"][:, slot, :]
+                t_["sig_in", q, g] = dst
+            else:
+                dst = staged(("sig_in", q, g))
             raw = t_["sig_raw", q, g // 2][:, :, (g % 2) * GROUP : (g % 2 + 1) * GROUP]
-            copy = nc.scalar.copy if on_scalar else nc.vector.tensor_copy
-            copy(
-                out=dst[:].rearrange("p (t m j) -> p m j t", t=PACK, j=PACK),
-                in_=raw.rearrange("p j (m t) -> p m j t", t=PACK),
-            )
+            dst = dst[:].rearrange("p (t m j) -> p m j t", t=PACK, j=PACK)
+            src = raw.rearrange("p j (m t) -> p m j t", t=PACK)
+            if engine == "vector":
+                nc.vector.tensor_copy(out=dst, in_=src)
+            elif engine == "scalar":
+                nc.scalar.copy(out=dst, in_=src)
+            else:
+                nc.gpsimd.tensor_scalar(out=dst, in0=src, scalar1=1.0, scalar2=0.0, op0=MULT, op1=ADD)
 
         def signal_pass(g, c, t, q):
             if q == 0:
@@ -243,27 +259,28 @@ def tile_receptor_occupancy_transcription_h3_kernel(
         def quantise_y(g, c, w0, w1):
             if w0 == 0:
                 t_["y_codes", g, c] = ywords.tile([P, HALF], U32, name="y_codes", tag="ywords", align_bytes=64)
-            if w0 == 0 and c == 0:
-                t_["y_scales", g] = keep.tile([P, C], U8, name="y_scales_%d" % g, align_bytes=64)
             codes = t_["y_codes", g, c][:, w0:w1]
             nc.vector.quantize_mx(
                 out=codes.bitcast(FP8X4),
-                scales=t_["y_scales", g][:, c * HALF + w0 : c * HALF + w1],
+                scales=y_scales[:, g, c * HALF + w0 : c * HALF + w1],
                 in_=t_["y_in", g, c][:, w0 * PACK : w1 * PACK],
             )
             words = out_1[g].rearrange("p w t -> p (w t)").bitcast(I32)
             nc.sync.dma_start(out=words[:, c * HALF + w0 : c * HALF + w1], in_=codes.bitcast(I32))
 
-        def store_scales(g):
+        def store_scales(g0, g1, c, last=False):
+            wells = slice(c * HALF, (c + 1) * HALF)
             for quad in range(4):
-                nc.sync.dma_start(
-                    out=out_2[g, 4 * quad : 4 * quad + 4, :].bitcast(I32),
-                    in_=t_["y_scales", g][32 * quad : 32 * quad + 4, :].bitcast(I32),
+                queue = nc.scalar if last and quad % 2 == 1 else nc.sync
+                queue.dma_start(
+                    out=out_2[g0:g1, 4 * quad : 4 * quad + 4, wells].rearrange("g r w -> r g w").bitcast(I32),
+                    in_=y_scales[32 * quad : 32 * quad + 4, g0:g1, wells].bitcast(I32),
                 )
 
 
-        load_aff(0)
         load_doses(0)
+        load_aff(0, 0, 2)
+        load_aff(0, 2, 4)
         load_aff(1)
         load_aff(2)
         load_sig(0, 0)
@@ -276,15 +293,16 @@ def tile_receptor_occupancy_transcription_h3_kernel(
         for g in range(GQ - 1):
             load_access(g)
 
-        for pair in range(2):
-            turn_aff(0, pair)
-            empty_aff(0, pair)
         weave_doses(0)
+        turn_aff(0, 0)
+        empty_aff(0, 0)
+        turn_aff(0, 1)
+        quantise(("dos_in", 0), ("dos", 0))
+        empty_aff(0, 1)
+        quantise(("aff_in", 0), ("aff", 0))
         for pair in range(2):
             turn_aff(1, pair)
             empty_aff(1, pair)
-        quantise(("aff_in", 0), ("aff", 0))
-        quantise(("dos_in", 0), ("dos", 0))
         def quantise_sig(q, g):
             quantise(("sig_in", q, g), ("sig", q, g))
 
@@ -294,50 +312,52 @@ def tile_receptor_occupancy_transcription_h3_kernel(
         drive(0, 0, 0)
         drive(0, 0, 1)
         quantise(("aff_in", 1), ("aff", 1))
-        for pair in range(2):
-            turn_aff(2, pair)
-            empty_aff(2, pair)
         drive(0, 0, 2)
         drive(0, 0, 3)
         weave_sig(0, 0)
-        quantise(("aff_in", 2), ("aff", 2))
+        for pair in range(2):
+            turn_aff(2, pair)
+            empty_aff(2, pair)
         weave_doses(1)
-        quantise_sig(0, 0)
-        weave_sig(0, 1)
+        quantise(("aff_in", 2), ("aff", 2))
         quantise(("dos_in", 1), ("dos", 1))
+        weave_sig(0, 1)
+        quantise_sig(0, 0)
         for q, c in [(1, 0), (2, 0), (0, 1), (1, 1), (2, 1)]:
             for b in range(4):
                 drive(q, c, b)
         turn_vecs()
 
-        sig_steps = [(0, 1), (1, 0), (1, 1), (2, 0), (2, 1), (0, 2)]
+        sig_steps = [(0, 1), (1, 0), (1, 1), (2, 0), (2, 1), (0, 2), (1, 2)]
         for i in range(1, len(sig_steps) + 1):
             if i < len(sig_steps):
-                weave_sig(*sig_steps[i])
+                weave_sig(*sig_steps[i], slot=(0 if i == len(sig_steps) - 1 else None))
             else:
                 empty_vecs()
             quantise_sig(*sig_steps[i - 1])
         load_access(GQ - 1)
 
-        tiles = [(0, 0), (1, 0), (2, 0), (0, 1), (1, 1), (2, 1), (3, 0), (3, 1)]
+        tiles = TILES
         for c in range(CH):
             for q in range(RQ):
                 saturate(q, c)
-        occupy(0, 0)
-        occupy(1, 0)
-        quantise_h(0, 0)
-        occupy(2, 0)
-        quantise_h(1, 0)
-        weave_sig(1, 2)
-        quantise_h(2, 0)
-        weave_sig(2, 2)
-        quantise_sig(1, 2)
-        occupy(0, 1)
+        weave_sig(2, 2, "gpsimd", 0)
+        weave_sig(0, 3, "gpsimd", 1)
+        for q in range(RQ):
+            occupy(q, 0)
+        for q in range(RQ):
+            quantise_h(q, 0)
         quantise_sig(2, 2)
+        quantise_sig(0, 3)
+        weave_sig(1, 3, "gpsimd", 0)
+        weave_sig(2, 3, "gpsimd", 1)
+        for q in range(RQ):
+            occupy(q, 1)
         for q in range(RQ):
             for t in range(PACK):
                 signal_pass(0, 0, t, q)
-        for t in range(PACK):
+        ahead = 7
+        for t in range(ahead - PACK):
             for q in range(RQ):
                 signal_pass(*tiles[1], t, q)
 
@@ -347,8 +367,10 @@ def tile_receptor_occupancy_transcription_h3_kernel(
         def finish(i):
             def run():
                 quantise_y(*tiles[i], 0, HALF)
-                if tiles[i][1] == CH - 1:
-                    store_scales(tiles[i][0])
+                if i == GQ - 1:
+                    store_scales(0, GQ, 0)
+                if i == len(tiles) - 2:
+                    store_scales(0, GQ - 1, 1)
             return run
 
         def job(fn, *args):
@@ -356,19 +378,18 @@ def tile_receptor_occupancy_transcription_h3_kernel(
 
         extras = {
 
-            (0, 3): [job(occupy, 1, 1), job(quantise_h, 0, 1)],
-            (1, 3): [job(occupy, 2, 1), job(quantise_h, 1, 1)],
-            (2, 0): [job(quantise_h, 2, 1)],
-            (2, 3): [cast(0, 0, True), cast(0, 1, True), job(weave_sig, 0, 3, True), cast(1, 0, True), cast(1, 1, True), finish(0), job(weave_sig, 1, 3), job(quantise_sig, 0, 3), finish(1)],
-            (3, 1): [cast(2, 0, True)],
-            (3, 3): [cast(2, 1, True), job(weave_sig, 2, 3), job(quantise_sig, 1, 3), finish(2), job(quantise_sig, 2, 3)],
-            (4, 1): [cast(3, 0, True)],
-            (4, 3): [cast(3, 1, True)],
-            (5, 0): [finish(3)],
-            (5, 3): [cast(4, 0, True)],
-            (6, 1): [cast(5, 0, False)],
-            (6, 3): [cast(4, 1, True), cast(5, 1, False), finish(4), finish(5)],
-            (7, 1): [cast(6, 0, False)],
+            (0, 3): [job(quantise_sig, 1, 3), job(quantise_sig, 2, 3)],
+            (1, 3): [job(quantise_h, 0, 1), job(quantise_h, 1, 1), job(quantise_h, 2, 1)],
+            (2, 3): [cast(0, 0, True), cast(0, 1, True)],
+            (3, 1): [finish(0), cast(1, 0, True)],
+            (3, 3): [cast(1, 1, True)],
+            (4, 1): [cast(2, 0, True), finish(1)],
+            (4, 3): [cast(2, 1, True), cast(3, 0, False)],
+            (5, 1): [cast(3, 1, True), finish(2)],
+            (5, 3): [cast(4, 0, True), finish(3), cast(4, 1, False)],
+            (6, 1): [finish(4)],
+            (6, 3): [cast(5, 0, True), cast(5, 1, False)],
+            (7, 1): [finish(5), cast(6, 0, False)],
             (7, 3): [cast(6, 1, True)],
 
         }
@@ -381,17 +402,14 @@ def tile_receptor_occupancy_transcription_h3_kernel(
                     store_y(g, c, t - 1, t + 1)
                 for extra in extras.get((i, t), []):
                     extra()
-                if i + 1 in LATE and t == 0:
-                    for tt in range(PACK):
-                        for q in range(RQ):
-                            signal_pass(*tiles[i + 1], tt, q)
-                if i + 2 < n and i + 2 not in LATE:
+                nxt = i * PACK + t + ahead
+                if nxt < n * PACK:
                     for q in range(RQ):
-                        signal_pass(*tiles[i + 2], t, q)
+                        signal_pass(*tiles[nxt // PACK], nxt % PACK, q)
         g, c = tiles[-1]
         round_y(g, c, 0, False)
         round_y(g, c, 1, True)
         finish(n - 2)()
         quantise_y(g, c, 0, HALF // 2)
         quantise_y(g, c, HALF // 2, HALF)
-        store_scales(g)
+        store_scales(g, g + 1, c, last=True)

@@ -24,7 +24,7 @@ RQ = R // GROUP
 GQ = G // GROUP
 CH = C // HALF
 VEC_ROWS = 12
-TILES = [(0, 0), (1, 0), (2, 0), (3, 0), (0, 1), (1, 1), (2, 1), (3, 1)]
+TILES = [(0, 0), (1, 0), (2, 0), (0, 1), (1, 1), (2, 1), (3, 0), (3, 1)]
 TINY = 2.0 ** -60
 
 
@@ -34,7 +34,7 @@ def tile_receptor_occupancy_transcription_h3_kernel(
     nc = tc.nc
     with ExitStack() as ctx:
         keep = ctx.enter_context(tc.tile_pool(name="keep", bufs=1))
-        small = ctx.enter_context(tc.tile_pool(name="small", bufs=7))
+        small = ctx.enter_context(tc.tile_pool(name="small", bufs=8))
         large = ctx.enter_context(tc.tile_pool(name="large", bufs=9))
         wide = ctx.enter_context(tc.tile_pool(name="wide", bufs=7))
         ywords = ctx.enter_context(tc.tile_pool(name="ywords", bufs=3))
@@ -64,6 +64,7 @@ def tile_receptor_occupancy_transcription_h3_kernel(
         tiny = keep.tile([P, 1], F32, name="tiny")
         warm = keep.tile([P, 1], F32, name="warm")
         y_scales = keep.tile([P, GQ, C], U8, name="y_scales", align_bytes=64)
+        square = keep.tile([P, P], F32, name="square")
         rows = keep.tile([P, GROUP], BF16, name="rows")
         vecs = keep.tile([P, VEC_ROWS, PACK], BF16, name="vecs")
         bas = vecs[:, 4 : 4 + GQ, :]
@@ -71,6 +72,7 @@ def tile_receptor_occupancy_transcription_h3_kernel(
         nc.gpsimd.memset(tiny[:], TINY)
         make_identity(nc, ident[:])
         nc.gpsimd.memset(rows[:].bitcast(I32), 0)
+        nc.gpsimd.memset(square[:], 0.0)
         nc.scalar.activation(out=warm[:], in_=tiny[:], func=ACT.Ln, bias=tiny[:])
 
         def load_aff(q, t0=0, t1=PACK):
@@ -113,7 +115,7 @@ def tile_receptor_occupancy_transcription_h3_kernel(
 
         def turn_vecs():
             words = rows[:].bitcast(F32)
-            bank = psum_vecs.tile([P, 2, P], F32, name="vec_bank")
+            bank = psum_vecs.tile([P, 2, P], F32, name="vec_bank", tag="vec_bank")
             for u in range(2):
                 nc.tensor.transpose(bank[:, u, :], words[:, u : GROUP // 2 : 2], ident[:])
             t_["vec_bank"] = bank
@@ -124,6 +126,17 @@ def tile_receptor_occupancy_transcription_h3_kernel(
                 out=vecs[:].rearrange("p r t -> p (r t)").bitcast(F32).rearrange("p (r u) -> p r u", u=2),
                 in_=bank[:, :, 0:VEC_ROWS].rearrange("p u r -> p r u"),
             )
+
+        def widen_density():
+            nc.vector.tensor_copy(out=square[:, 0 : RQ * PACK], in_=vecs[:, 0:RQ, :].rearrange("p r t -> p (r t)"))
+
+        def turn_density():
+            bank = psum_vecs.tile([P, P], F32, name="vec_bank", tag="vec_bank")
+            nc.tensor.transpose(bank[:], square[:], ident[:])
+            turned = keep.tile([P, P], F32, name="turned")
+            nc.vector.tensor_copy(out=turned[:], in_=bank[:])
+            t_["density"] = psum_vecs.tile([P, P], F32, name="vec_bank", tag="vec_bank")
+            nc.tensor.transpose(t_["density"][:], turned[:], ident[:])
 
         def turn_aff(q, pair):
             words = t_["aff_raw", q][:].bitcast(F32).rearrange("p (t w) -> p t w", t=PACK)
@@ -178,20 +191,16 @@ def tile_receptor_occupancy_transcription_h3_kernel(
 
         def occupy(q, c):
             dst = staged(("h_in", q, c))
-            pairs = t_["vec_bank"][:].rearrange("p u r -> p (u r)").bitcast(BF16)
-            dens = pairs.rearrange("p (u r e) -> p r u e", u=2, e=2)[:, q : q + 1, :, :]
             nc.vector.tensor_tensor(
-                out=dst[:].rearrange("p (w u e) -> p w u e", u=2, e=2),
-                in0=t_["bound", q, c][:].rearrange("p w (u e) -> p w u e", u=2),
-                in1=dens.to_broadcast([P, HALF, 2, 2]),
+                out=dst[:].rearrange("p (w t) -> p w t", t=PACK),
+                in0=t_["bound", q, c][:],
+                in1=t_["density"][:, q * PACK : (q + 1) * PACK].unsqueeze(1).to_broadcast([P, HALF, PACK]),
                 op=MULT,
             )
 
         def weave_sig(q, g, engine="vector", slot=None):
-            if slot == 0:
-                t_["relay"] = relay.tile([P, 2, GROUP * PACK], BF16, name="relay", tag="relay", align_bytes=64)
             if slot is not None:
-                dst = t_["relay"][:, slot, :]
+                dst = relay.tile([P, GROUP * PACK], BF16, name="relay", tag="relay", align_bytes=64)
                 t_["sig_in", q, g] = dst
             else:
                 dst = staged(("sig_in", q, g))
@@ -268,8 +277,8 @@ def tile_receptor_occupancy_transcription_h3_kernel(
             words = out_1[g].rearrange("p w t -> p (w t)").bitcast(I32)
             nc.sync.dma_start(out=words[:, c * HALF + w0 : c * HALF + w1], in_=codes.bitcast(I32))
 
-        def store_scales(g0, g1, c, last=False):
-            wells = slice(c * HALF, (c + 1) * HALF)
+        def store_scales(g0, g1, last=False):
+            wells = slice(0, C)
             for quad in range(4):
                 queue = nc.scalar if last and quad % 2 == 1 else nc.sync
                 queue.dma_start(
@@ -326,40 +335,52 @@ def tile_receptor_occupancy_transcription_h3_kernel(
         for q, c in [(1, 0), (2, 0), (0, 1), (1, 1), (2, 1)]:
             for b in range(4):
                 drive(q, c, b)
-        turn_vecs()
+            if (q, c) == (0, 1):
+                turn_vecs()
 
-        sig_steps = [(0, 1), (1, 0), (1, 1), (2, 0), (2, 1), (0, 2), (1, 2)]
-        for i in range(1, len(sig_steps) + 1):
-            if i < len(sig_steps):
-                weave_sig(*sig_steps[i], slot=(0 if i == len(sig_steps) - 1 else None))
-            else:
-                empty_vecs()
-            quantise_sig(*sig_steps[i - 1])
+        weave_sig(1, 0)
+        quantise_sig(0, 1)
+        weave_sig(1, 1)
+        quantise_sig(1, 0)
+        weave_sig(2, 0)
+        quantise_sig(1, 1)
+        empty_vecs()
+        weave_sig(2, 1)
+        widen_density()
+        quantise_sig(2, 0)
+        weave_sig(0, 2)
+        turn_density()
+        quantise_sig(2, 1)
+        weave_sig(1, 2, slot=0)
+        quantise_sig(0, 2)
+        quantise_sig(1, 2)
         load_access(GQ - 1)
 
         tiles = TILES
+        ahead = 7
+        quarters = [(g, c, t) for g, c in tiles for t in range(PACK)]
         for c in range(CH):
             for q in range(RQ):
                 saturate(q, c)
         weave_sig(2, 2, "gpsimd", 0)
-        weave_sig(0, 3, "gpsimd", 1)
-        for q in range(RQ):
-            occupy(q, 0)
-        for q in range(RQ):
+        occupy(0, 0)
+        occupy(1, 0)
+        for q in range(2):
             quantise_h(q, 0)
+            for quarter in quarters[:ahead]:
+                signal_pass(*quarter, q)
         quantise_sig(2, 2)
+        weave_sig(0, 3, "gpsimd", 0)
+        occupy(2, 0)
+        occupy(0, 1)
+        quantise_h(2, 0)
+        for quarter in quarters[:ahead]:
+            signal_pass(*quarter, 2)
+        quantise_h(0, 1)
         quantise_sig(0, 3)
         weave_sig(1, 3, "gpsimd", 0)
-        weave_sig(2, 3, "gpsimd", 1)
-        for q in range(RQ):
-            occupy(q, 1)
-        for q in range(RQ):
-            for t in range(PACK):
-                signal_pass(0, 0, t, q)
-        ahead = 7
-        for t in range(ahead - PACK):
-            for q in range(RQ):
-                signal_pass(*tiles[1], t, q)
+        occupy(1, 1)
+        occupy(2, 1)
 
         def cast(i, part, on_scalar):
             return lambda: round_y(*tiles[i], part, on_scalar)
@@ -367,10 +388,10 @@ def tile_receptor_occupancy_transcription_h3_kernel(
         def finish(i):
             def run():
                 quantise_y(*tiles[i], 0, HALF)
-                if i == GQ - 1:
-                    store_scales(0, GQ, 0)
-                if i == len(tiles) - 2:
-                    store_scales(0, GQ - 1, 1)
+                if i == 4:
+                    store_scales(0, 2)
+                if i == 5:
+                    store_scales(2, 3)
             return run
 
         def job(fn, *args):
@@ -378,18 +399,17 @@ def tile_receptor_occupancy_transcription_h3_kernel(
 
         extras = {
 
-            (0, 3): [job(quantise_sig, 1, 3), job(quantise_sig, 2, 3)],
-            (1, 3): [job(quantise_h, 0, 1), job(quantise_h, 1, 1), job(quantise_h, 2, 1)],
+            (0, 3): [job(quantise_h, 1, 1), job(quantise_h, 2, 1)],
             (2, 3): [cast(0, 0, True), cast(0, 1, True)],
             (3, 1): [finish(0), cast(1, 0, True)],
-            (3, 3): [cast(1, 1, True)],
-            (4, 1): [cast(2, 0, True), finish(1)],
-            (4, 3): [cast(2, 1, True), cast(3, 0, False)],
-            (5, 1): [cast(3, 1, True), finish(2)],
-            (5, 3): [cast(4, 0, True), finish(3), cast(4, 1, False)],
+            (3, 3): [cast(1, 1, True), job(quantise_sig, 1, 3), job(weave_sig, 2, 3)],
+            (4, 1): [cast(2, 0, True), job(quantise_sig, 2, 3), finish(1)],
+            (4, 3): [cast(2, 1, True)],
+            (5, 1): [cast(3, 0, True), finish(2)],
+            (5, 3): [cast(3, 1, True), cast(4, 0, False), cast(4, 1, False), finish(3)],
             (6, 1): [finish(4)],
             (6, 3): [cast(5, 0, True), cast(5, 1, False)],
-            (7, 1): [finish(5), cast(6, 0, False)],
+            (7, 1): [cast(6, 0, False), finish(5)],
             (7, 3): [cast(6, 1, True)],
 
         }
@@ -412,4 +432,4 @@ def tile_receptor_occupancy_transcription_h3_kernel(
         finish(n - 2)()
         quantise_y(g, c, 0, HALF // 2)
         quantise_y(g, c, HALF // 2, HALF)
-        store_scales(g, g + 1, c, last=True)
+        store_scales(g, g + 1, last=True)

@@ -22,10 +22,15 @@ GROUP = P * PACK
 HALF = 512
 RQ = R // GROUP
 GQ = G // GROUP
-CH = C // HALF
-VEC_ROWS = 12
+RUN = 4
+TINY = 2.0**-60
+
+DENSITY_ROW, BASAL_ROW, VMAX_ROW, VECTOR_ROWS = 0, 4, 8, 12
+
+BANKS = 7
+
 TILES = [(0, 0), (1, 0), (2, 0), (0, 1), (1, 1), (2, 1), (3, 0), (3, 1)]
-TINY = 2.0 ** -60
+QUARTERS = [(g, c, t) for g, c in TILES for t in range(PACK)]
 
 
 def tile_receptor_occupancy_transcription_h3_kernel(
@@ -34,402 +39,373 @@ def tile_receptor_occupancy_transcription_h3_kernel(
     nc = tc.nc
     with ExitStack() as ctx:
         keep = ctx.enter_context(tc.tile_pool(name="keep", bufs=1))
-        small = ctx.enter_context(tc.tile_pool(name="small", bufs=8))
-        large = ctx.enter_context(tc.tile_pool(name="large", bufs=9))
+        stage = ctx.enter_context(tc.tile_pool(name="stage", bufs=8))
+        loads = ctx.enter_context(tc.tile_pool(name="loads", bufs=9))
         wide = ctx.enter_context(tc.tile_pool(name="wide", bufs=7))
-        ywords = ctx.enter_context(tc.tile_pool(name="ywords", bufs=3))
-        psum = ctx.enter_context(tc.psum_pool(name="psum", bufs=7))
-        psum_vecs = ctx.enter_context(tc.psum_pool(name="psum_vecs", bufs=1))
+        y_words = ctx.enter_context(tc.tile_pool(name="y_words", bufs=3))
+        psum = ctx.enter_context(tc.psum_pool(name="psum", bufs=BANKS))
+        psum_vectors = ctx.enter_context(tc.psum_pool(name="psum_vectors", bufs=1))
         relay = ctx.enter_context(tc.tile_pool(name="relay", bufs=1))
         ctx.enter_context(tc.manual_schedule())
 
-        t_ = {}
+        live = {}
 
         def staged(key):
-            t_[key] = small.tile([P, GROUP * PACK], BF16, name="staged", tag="small", align_bytes=64)
-            return t_[key]
+            live[key] = stage.tile([P, GROUP * PACK], BF16, name="staged", tag="stage", align_bytes=64)
+            return live[key]
 
-        def operand(key, width):
-            name = "_".join(str(k) for k in key)
-            codes = keep.tile([P, width], U32, name="codes_" + name, align_bytes=64)
-            scales = keep.tile([P, width], U8, name="scales_" + name, align_bytes=64)
-            t_[key] = (codes, scales)
-            return t_[key]
+        def quantise(name, *index):
+            label = "_".join([name] + [str(i) for i in index])
+            codes = keep.tile([P, GROUP], U32, name="codes_" + label, align_bytes=64)
+            scales = keep.tile([P, GROUP], U8, name="scales_" + label, align_bytes=64)
+            live[(name,) + index] = (codes, scales)
+            nc.vector.quantize_mx(
+                out=codes[:].bitcast(FP8X4), scales=scales[:], in_=live[(name + "_in",) + index][:]
+            )
 
-        def quantise(src_key, dst_key):
-            codes, scales = operand(dst_key, GROUP)
-            nc.vector.quantize_mx(out=codes[:].bitcast(FP8X4), scales=scales[:], in_=t_[src_key][:])
+        def multiply(out, stationary, columns, moving, wells, start, stop):
+            nc.tensor.matmul_mx(
+                out=out,
+                lhsT=stationary[0][:, columns].bitcast(FP8X4),
+                lhsT_scale=stationary[1][:, columns],
+                rhs=moving[0][:, wells].bitcast(FP8X4),
+                rhs_scale=moving[1][:, wells],
+                start=start,
+                stop=stop,
+            )
 
         ident = keep.tile([P, P], F32, name="ident")
         tiny = keep.tile([P, 1], F32, name="tiny")
-        warm = keep.tile([P, 1], F32, name="warm")
-        y_scales = keep.tile([P, GQ, C], U8, name="y_scales", align_bytes=64)
-        square = keep.tile([P, P], F32, name="square")
-        rows = keep.tile([P, GROUP], BF16, name="rows")
-        vecs = keep.tile([P, VEC_ROWS, PACK], BF16, name="vecs")
-        bas = vecs[:, 4 : 4 + GQ, :]
-        vm = vecs[:, 8 : 8 + GQ, :]
+        one = keep.tile([P, 1], F32, name="one")
+        zero = keep.tile([P, 1], F32, name="zero")
+        y_scales = keep.tile([P, C], U8, name="y_scales", align_bytes=64)
+        vector_rows = keep.tile([P, GROUP], BF16, name="rows")
+        vectors = keep.tile([P, VECTOR_ROWS, PACK], BF16, name="vectors")
+        density_wide = keep.tile([P, P], F32, name="density_wide")
+        nc.gpsimd.memset(one[:], 1.0)
         nc.gpsimd.memset(tiny[:], TINY)
         make_identity(nc, ident[:])
-        nc.gpsimd.memset(rows[:].bitcast(I32), 0)
-        nc.gpsimd.memset(square[:], 0.0)
-        nc.scalar.activation(out=warm[:], in_=tiny[:], func=ACT.Ln, bias=tiny[:])
+        nc.gpsimd.memset(vector_rows[:].bitcast(I32), 0)
+        nc.gpsimd.memset(density_wide[:], 0.0)
+        nc.scalar.activation(out=zero[:], in_=one[:], func=ACT.Ln)
 
-        def load_aff(q, t0=0, t1=PACK):
+
+        def load_affinity(q, t0=0, t1=PACK):
             if t0 == 0:
                 staged(("aff_raw", q))
             nc.sync.dma_start(
-                out=t_["aff_raw", q][:].rearrange("p (t k) -> p t k", t=PACK)[:, t0:t1, :],
+                out=live["aff_raw", q][:].rearrange("p (t k) -> p t k", t=PACK)[:, t0:t1, :],
                 in_=affinity[q * GROUP : (q + 1) * GROUP, :].rearrange("(m t) k -> m t k", t=PACK)[:, t0:t1, :],
             )
 
         def load_doses(c):
-            raw = staged(("dos_raw", c))
             nc.sync.dma_start(
-                out=raw[:].rearrange("p (j w) -> p j w", j=PACK),
+                out=staged(("dos_raw", c))[:].rearrange("p (j w) -> p j w", j=PACK),
                 in_=doses[:, c * HALF : (c + 1) * HALF].rearrange("(p j) w -> p j w", j=PACK),
             )
 
-        def load_sig(q, gg):
-            raw = large.tile([P, PACK, 2 * GROUP], BF16, name="sig_raw", tag="large")
-            t_["sig_raw", q, gg] = raw
-            nc.sync.dma_start(
-                out=raw[:],
-                in_=signalling[q * GROUP : (q + 1) * GROUP, gg * 2 * GROUP : (gg + 1) * 2 * GROUP].rearrange(
-                    "(p j) w -> p j w", j=PACK
-                ),
-            )
+        def load_signalling(q, pair):
+            raw = loads.tile([P, PACK, 2 * GROUP], BF16, name="sig_raw", tag="loads")
+            live["sig_raw", q, pair] = raw
+            block = signalling[q * GROUP : (q + 1) * GROUP, pair * 2 * GROUP : (pair + 1) * 2 * GROUP]
+            nc.sync.dma_start(out=raw[:], in_=block.rearrange("(p j) w -> p j w", j=PACK))
 
         def load_access(g):
-            raw = large.tile([P, PACK, C], BF16, name="acc_raw", tag="large")
-            t_["access", g] = raw
+            raw = loads.tile([P, PACK, C], BF16, name="access", tag="loads")
+            live["access", g] = raw
             nc.sync.dma_start(
                 out=raw[:], in_=access[g * GROUP : (g + 1) * GROUP, :].rearrange("(p t) w -> p t w", t=PACK)
             )
 
-        def load_vecs():
-            for first, vec, q0, q1 in [(0, density, 0, 2), (2, density, 2, 3), (4, basal, 0, GQ), (8, vmax, 0, GQ)]:
+        def load_vectors():
+            pieces = [
+                (DENSITY_ROW, density, 0, 2),
+                (DENSITY_ROW, density, 2, RQ),
+                (BASAL_ROW, basal, 0, GQ),
+                (VMAX_ROW, vmax, 0, GQ),
+            ]
+            for row, vector, q0, q1 in pieces:
                 nc.sync.dma_start(
-                    out=rows[first : first + q1 - q0, :], in_=vec.rearrange("(q k) -> q k", k=GROUP)[q0:q1, :]
+                    out=vector_rows[row + q0 : row + q1, :], in_=vector.rearrange("(q k) -> q k", k=GROUP)[q0:q1, :]
                 )
 
-        def turn_vecs():
-            words = rows[:].bitcast(F32)
-            bank = psum_vecs.tile([P, 2, P], F32, name="vec_bank", tag="vec_bank")
+
+        def turn_vectors():
+            words = vector_rows[:].bitcast(F32)
+            bank = psum_vectors.tile([P, 2, P], F32, name="vector_bank", tag="vector_bank")
+            live["vector_bank"] = bank
             for u in range(2):
                 nc.tensor.transpose(bank[:, u, :], words[:, u : GROUP // 2 : 2], ident[:])
-            t_["vec_bank"] = bank
 
-        def empty_vecs():
-            bank = t_["vec_bank"]
+        def empty_vectors():
             nc.vector.tensor_copy(
-                out=vecs[:].rearrange("p r t -> p (r t)").bitcast(F32).rearrange("p (r u) -> p r u", u=2),
-                in_=bank[:, :, 0:VEC_ROWS].rearrange("p u r -> p r u"),
+                out=vectors[:].rearrange("p r t -> p (r t)").bitcast(F32).rearrange("p (r u) -> p r u", u=2),
+                in_=live["vector_bank"][:, :, 0:VECTOR_ROWS].rearrange("p u r -> p r u"),
             )
 
         def widen_density():
-            nc.vector.tensor_copy(out=square[:, 0 : RQ * PACK], in_=vecs[:, 0:RQ, :].rearrange("p r t -> p (r t)"))
+            nc.vector.tensor_copy(
+                out=density_wide[:, 0 : RQ * PACK],
+                in_=vectors[:, DENSITY_ROW : DENSITY_ROW + RQ, :].rearrange("p r t -> p (r t)"),
+            )
 
-        def turn_density():
-            bank = psum_vecs.tile([P, P], F32, name="vec_bank", tag="vec_bank")
-            nc.tensor.transpose(bank[:], square[:], ident[:])
-            turned = keep.tile([P, P], F32, name="turned")
+        def density_to_psum():
+            bank = psum_vectors.tile([P, P], F32, name="vector_bank", tag="vector_bank")
+            nc.tensor.transpose(bank[:], density_wide[:], ident[:])
+            turned = keep.tile([P, P], F32, name="density_turned")
             nc.vector.tensor_copy(out=turned[:], in_=bank[:])
-            t_["density"] = psum_vecs.tile([P, P], F32, name="vec_bank", tag="vec_bank")
-            nc.tensor.transpose(t_["density"][:], turned[:], ident[:])
+            live["density"] = psum_vectors.tile([P, P], F32, name="vector_bank", tag="vector_bank")
+            nc.tensor.transpose(live["density"][:], turned[:], ident[:])
 
-        def turn_aff(q, pair):
-            words = t_["aff_raw", q][:].bitcast(F32).rearrange("p (t w) -> p t w", t=PACK)
+
+        def turn_affinity(q, pair):
+            words = live["aff_raw", q][:].bitcast(F32).rearrange("p (t w) -> p t w", t=PACK)
             bank = psum.tile([P, 2, 2, P], F32, name="bank", tag="bank")
-            t_["aff_bank", q, pair] = bank
-            for tt in range(2):
+            live["aff_bank", q, pair] = bank
+            for t in range(2):
                 for u in range(2):
-                    nc.tensor.transpose(bank[:, tt, u, :], words[:, 2 * pair + tt, u : L // 2 : 2], ident[:])
+                    nc.tensor.transpose(bank[:, t, u, :], words[:, 2 * pair + t, u : L // 2 : 2], ident[:])
 
-        def empty_aff(q, pair):
-            if ("aff_in", q) not in t_:
+        def empty_affinity(q, pair, copy):
+            if pair == 0:
                 staged(("aff_in", q))
-            dst = t_["aff_in", q][:].bitcast(F32).rearrange("p (t m u) -> p t m u", t=PACK, u=2)
-            copy = nc.vector.tensor_copy if pair == 1 and q < 2 else nc.scalar.copy
+            words = live["aff_in", q][:].bitcast(F32).rearrange("p (t m u) -> p t m u", t=PACK, u=2)
             copy(
-                out=dst[:, 2 * pair : 2 * pair + 2, :, :],
-                in_=t_["aff_bank", q, pair][:].rearrange("p t u m -> p t m u"),
+                out=words[:, 2 * pair : 2 * pair + 2, :, :],
+                in_=live["aff_bank", q, pair][:].rearrange("p t u m -> p t m u"),
             )
 
         def weave_doses(c):
-            dst = staged(("dos_in", c))
             nc.vector.tensor_copy(
-                out=dst[:].rearrange("p (w i j) -> p w j i", i=4, j=PACK),
-                in_=t_["dos_raw", c][:].rearrange("p (j w i) -> p w j i", j=PACK, i=4),
+                out=staged(("dos_in", c))[:].rearrange("p (w i j) -> p w j i", i=RUN, j=PACK),
+                in_=live["dos_raw", c][:].rearrange("p (j w i) -> p w j i", j=PACK, i=RUN),
             )
 
         def drive(q, c, b):
             bank = psum.tile([P, PACK, P], F32, name="bank", tag="bank")
-            a_codes, a_scales = t_["aff", q]
-            d_codes, d_scales = t_["dos", c]
             wells = slice(b * P, (b + 1) * P)
             for t in range(PACK):
-                cols = slice(t * P, (t + 1) * P)
-                nc.tensor.matmul_mx(
-                    out=bank[:, t, :],
-                    lhsT=a_codes[:, cols].bitcast(FP8X4),
-                    lhsT_scale=a_scales[:, cols],
-                    rhs=d_codes[:, wells].bitcast(FP8X4),
-                    rhs_scale=d_scales[:, wells],
-                    start=True,
-                    stop=True,
-                )
+                multiply(bank[:, t, :], live["aff", q], slice(t * P, (t + 1) * P), live["dos", c], wells, True, True)
             if b == 0:
-                t_["bound", q, c] = wide.tile([P, HALF, PACK], F32, name="bound", tag="wide")
+                live["bound", q, c] = wide.tile([P, HALF, PACK], F32, name="bound", tag="wide")
             nc.scalar.activation(
-                out=t_["bound", q, c][:, wells, :], in_=bank[:].rearrange("p t w -> p w t"), func=ACT.Ln, bias=tiny[:]
+                out=live["bound", q, c][:, wells, :], in_=bank[:].rearrange("p t w -> p w t"), func=ACT.Ln, bias=tiny[:]
             )
 
         def saturate(q, c):
-            bound = t_["bound", q, c]
-            nc.scalar.activation(out=bound[:], in_=bound[:], func=ACT.Sigmoid)
+            bound = live["bound", q, c]
+            nc.scalar.activation(out=bound[:], in_=bound[:], func=ACT.Sigmoid, bias=zero[:])
 
         def occupy(q, c):
-            dst = staged(("h_in", q, c))
             nc.vector.tensor_tensor(
-                out=dst[:].rearrange("p (w t) -> p w t", t=PACK),
-                in0=t_["bound", q, c][:],
-                in1=t_["density"][:, q * PACK : (q + 1) * PACK].unsqueeze(1).to_broadcast([P, HALF, PACK]),
+                out=staged(("h_in", q, c))[:].rearrange("p (w t) -> p w t", t=PACK),
+                in0=live["bound", q, c][:],
+                in1=live["density"][:, q * PACK : (q + 1) * PACK].unsqueeze(1).to_broadcast([P, HALF, PACK]),
                 op=MULT,
             )
 
-        def weave_sig(q, g, engine="vector", slot=None):
-            if slot is not None:
-                dst = relay.tile([P, GROUP * PACK], BF16, name="relay", tag="relay", align_bytes=64)
-                t_["sig_in", q, g] = dst
-            else:
-                dst = staged(("sig_in", q, g))
-            raw = t_["sig_raw", q, g // 2][:, :, (g % 2) * GROUP : (g % 2 + 1) * GROUP]
-            dst = dst[:].rearrange("p (t m j) -> p m j t", t=PACK, j=PACK)
-            src = raw.rearrange("p j (m t) -> p m j t", t=PACK)
-            if engine == "vector":
-                nc.vector.tensor_copy(out=dst, in_=src)
-            elif engine == "scalar":
-                nc.scalar.copy(out=dst, in_=src)
-            else:
-                nc.gpsimd.tensor_scalar(out=dst, in0=src, scalar1=1.0, scalar2=0.0, op0=MULT, op1=ADD)
 
-        def signal_pass(g, c, t, q):
+        def weave_signalling(q, g, engine, relayed=False):
+            if relayed:
+                live["sig_in", q, g] = relay.tile([P, GROUP * PACK], BF16, name="relay", tag="relay", align_bytes=64)
+            else:
+                staged(("sig_in", q, g))
+            woven = live["sig_in", q, g][:].rearrange("p (t m j) -> p t m j", t=PACK, j=PACK)
+            raw = live["sig_raw", q, g // 2][:, :, (g % 2) * GROUP : (g % 2 + 1) * GROUP]
+            raw = raw.rearrange("p j (m t) -> p t m j", t=PACK)
+            if engine == "gpsimd":
+                nc.gpsimd.tensor_scalar(out=woven, in0=raw, scalar1=1.0, scalar2=0.0, op0=MULT, op1=ADD)
+            else:
+                copy = nc.vector.tensor_copy if engine == "vector" else nc.scalar.copy
+                copy(out=woven.rearrange("p t m j -> p m j t"), in_=raw.rearrange("p t m j -> p m j t"))
+
+        def signal_pass(k, q):
+            g, c, t = QUARTERS[k]
             if q == 0:
-                t_["z", g, c, t] = psum.tile([P, HALF], F32, name="bank", tag="bank")
-            s_codes, s_scales = t_["sig", q, g]
-            h_codes, h_scales = t_["h", q, c]
-            cols = slice(t * P, (t + 1) * P)
-            nc.tensor.matmul_mx(
-                out=t_["z", g, c, t][:],
-                lhsT=s_codes[:, cols].bitcast(FP8X4),
-                lhsT_scale=s_scales[:, cols],
-                rhs=h_codes[:].bitcast(FP8X4),
-                rhs_scale=h_scales[:],
-                start=(q == 0),
-                stop=(q == RQ - 1),
-            )
+                live["z", k] = psum.tile([P, HALF], F32, name="bank", tag="bank")
+            columns = slice(t * P, (t + 1) * P)
+            multiply(live["z", k][:], live["sig", q, g], columns, live["h", q, c], slice(0, HALF), q == 0, q == RQ - 1)
 
-        def activate(g, c, t):
+        def transcribe(k):
+            g, c, t = QUARTERS[k]
             if t == 0:
-                t_["y", g, c] = wide.tile([P, PACK, HALF], F32, name="y", tag="wide")
+                live["y", g, c] = wide.tile([P, PACK, HALF], F32, name="y", tag="wide")
+            y = live["y", g, c][:, t, :]
             nc.scalar.activation(
-                out=t_["y", g, c][:, t, :], in_=t_["z", g, c, t][:], func=ACT.Sigmoid, bias=bas[:, g, t : t + 1]
+                out=y, in_=live["z", k][:], func=ACT.Sigmoid, bias=vectors[:, BASAL_ROW + g, t : t + 1]
             )
-
-        def transcribe(g, c, t):
-            y = t_["y", g, c][:, t, :]
             nc.vector.scalar_tensor_tensor(
                 out=y,
                 in0=y,
-                scalar=vm[:, g, t : t + 1],
-                in1=t_["access", g][:, t, c * HALF : (c + 1) * HALF],
+                scalar=vectors[:, VMAX_ROW + g, t : t + 1],
+                in1=live["access", g][:, t, c * HALF : (c + 1) * HALF],
                 op0=MULT,
                 op1=MULT,
             )
 
-        def store_y(g, c, t0, t1):
+        def store_y(k0, k1):
+            g, c, t0 = QUARTERS[k0]
+            values = slice(t0, QUARTERS[k1][2] + 1)
             rows = out_0[g * GROUP : (g + 1) * GROUP, c * HALF : (c + 1) * HALF].rearrange("(p t) w -> p t w", t=PACK)
-            nc.sync.dma_start(out=rows[:, t0:t1, :], in_=t_["y", g, c][:, t0:t1, :])
+            nc.sync.dma_start(out=rows[:, values, :], in_=live["y", g, c][:, values, :])
 
-        def round_y(g, c, part, on_scalar):
+        def round_y(i, part, copy):
+            g, c = TILES[i]
             if part == 0:
-                staged(("y_in", g, c))
-            half = HALF // 2
-            dst = t_["y_in", g, c][:, part * half * PACK : (part + 1) * half * PACK]
-            src = t_["y", g, c][:, :, part * half : (part + 1) * half]
-            dst = dst.rearrange("p (w i t) -> p w t i", i=4, t=PACK)
-            src = src.rearrange("p t (w i) -> p w t i", i=4)
-            if on_scalar:
-                nc.scalar.copy(out=dst, in_=src)
-            else:
-                nc.vector.tensor_copy(out=dst, in_=src)
+                staged(("y_in", i))
+            w0, w1 = part * HALF // 2, (part + 1) * HALF // 2
+            copy(
+                out=live["y_in", i][:, w0 * PACK : w1 * PACK].rearrange("p (w i t) -> p w t i", i=RUN, t=PACK),
+                in_=live["y", g, c][:, :, w0:w1].rearrange("p t (w i) -> p w t i", i=RUN),
+            )
 
-        def quantise_y(g, c, w0, w1):
+        def quantise_y(i, w0=0, w1=HALF):
+            g, c = TILES[i]
             if w0 == 0:
-                t_["y_codes", g, c] = ywords.tile([P, HALF], U32, name="y_codes", tag="ywords", align_bytes=64)
-            codes = t_["y_codes", g, c][:, w0:w1]
+                live["y_codes", i] = y_words.tile([P, HALF], U32, name="y_codes", tag="y_words", align_bytes=64)
+            codes = live["y_codes", i][:, w0:w1]
+            wells = slice(c * HALF + w0, c * HALF + w1)
             nc.vector.quantize_mx(
                 out=codes.bitcast(FP8X4),
-                scales=y_scales[:, g, c * HALF + w0 : c * HALF + w1],
-                in_=t_["y_in", g, c][:, w0 * PACK : w1 * PACK],
+                scales=y_scales[4 * g : P, wells],
+                in_=live["y_in", i][:, w0 * PACK : w1 * PACK],
             )
             words = out_1[g].rearrange("p w t -> p (w t)").bitcast(I32)
-            nc.sync.dma_start(out=words[:, c * HALF + w0 : c * HALF + w1], in_=codes.bitcast(I32))
+            nc.sync.dma_start(out=words[:, wells], in_=codes.bitcast(I32))
 
-        def store_scales(g0, g1, last=False):
-            wells = slice(0, C)
+        def store_scales():
             for quad in range(4):
-                queue = nc.scalar if last and quad % 2 == 1 else nc.sync
+                queue = nc.scalar if quad % 2 == 1 else nc.sync
                 queue.dma_start(
-                    out=out_2[g0:g1, 4 * quad : 4 * quad + 4, wells].rearrange("g r w -> r g w").bitcast(I32),
-                    in_=y_scales[32 * quad : 32 * quad + 4, g0:g1, wells].bitcast(I32),
+                    out=out_2[:, 4 * quad : 4 * quad + 4, :].bitcast(I32),
+                    in_=y_scales[32 * quad : 32 * quad + 4 * GQ, :].bitcast(I32),
                 )
 
+        on_scalar, on_vector = nc.scalar.copy, nc.vector.tensor_copy
 
         load_doses(0)
-        load_aff(0, 0, 2)
-        load_aff(0, 2, 4)
-        load_aff(1)
-        load_aff(2)
-        load_sig(0, 0)
+        load_affinity(0, 0, 2)
+        load_affinity(0, 2, PACK)
+        load_affinity(1)
+        load_affinity(2)
+        load_signalling(0, 0)
         load_doses(1)
-        load_sig(1, 0)
-        load_sig(2, 0)
-        load_vecs()
+        load_signalling(1, 0)
+        load_signalling(2, 0)
+        load_vectors()
         for q in range(RQ):
-            load_sig(q, 1)
+            load_signalling(q, 1)
         for g in range(GQ - 1):
             load_access(g)
 
         weave_doses(0)
-        turn_aff(0, 0)
-        empty_aff(0, 0)
-        turn_aff(0, 1)
-        quantise(("dos_in", 0), ("dos", 0))
-        empty_aff(0, 1)
-        quantise(("aff_in", 0), ("aff", 0))
-        for pair in range(2):
-            turn_aff(1, pair)
-            empty_aff(1, pair)
-        def quantise_sig(q, g):
-            quantise(("sig_in", q, g), ("sig", q, g))
-
-        def quantise_h(q, c):
-            quantise(("h_in", q, c), ("h", q, c))
-
+        turn_affinity(0, 0)
+        empty_affinity(0, 0, on_scalar)
+        turn_affinity(0, 1)
+        quantise("dos", 0)
+        empty_affinity(0, 1, on_vector)
+        quantise("aff", 0)
+        turn_affinity(1, 0)
+        empty_affinity(1, 0, on_scalar)
+        turn_affinity(1, 1)
+        empty_affinity(1, 1, on_vector)
         drive(0, 0, 0)
         drive(0, 0, 1)
-        quantise(("aff_in", 1), ("aff", 1))
+        quantise("aff", 1)
         drive(0, 0, 2)
         drive(0, 0, 3)
-        weave_sig(0, 0)
+        weave_signalling(0, 0, "vector")
         for pair in range(2):
-            turn_aff(2, pair)
-            empty_aff(2, pair)
+            turn_affinity(2, pair)
+            empty_affinity(2, pair, on_scalar)
         weave_doses(1)
-        quantise(("aff_in", 2), ("aff", 2))
-        quantise(("dos_in", 1), ("dos", 1))
-        weave_sig(0, 1)
-        quantise_sig(0, 0)
-        for q, c in [(1, 0), (2, 0), (0, 1), (1, 1), (2, 1)]:
-            for b in range(4):
+        quantise("aff", 2)
+        quantise("dos", 1)
+        weave_signalling(0, 1, "vector")
+        quantise("sig", 0, 0)
+        for q, c in [(1, 0), (2, 0), (0, 1)]:
+            for b in range(HALF // P):
                 drive(q, c, b)
-            if (q, c) == (0, 1):
-                turn_vecs()
+        turn_vectors()
+        for q, c in [(1, 1), (2, 1)]:
+            for b in range(HALF // P):
+                drive(q, c, b)
 
-        weave_sig(1, 0)
-        quantise_sig(0, 1)
-        weave_sig(1, 1)
-        quantise_sig(1, 0)
-        weave_sig(2, 0)
-        quantise_sig(1, 1)
-        empty_vecs()
-        weave_sig(2, 1)
+        weave_signalling(1, 0, "vector")
+        quantise("sig", 0, 1)
+        weave_signalling(1, 1, "vector")
+        quantise("sig", 1, 0)
+        weave_signalling(2, 0, "vector")
+        quantise("sig", 1, 1)
+        empty_vectors()
+        weave_signalling(2, 1, "vector")
         widen_density()
-        quantise_sig(2, 0)
-        weave_sig(0, 2)
-        turn_density()
-        quantise_sig(2, 1)
-        weave_sig(1, 2, slot=0)
-        quantise_sig(0, 2)
-        quantise_sig(1, 2)
+        quantise("sig", 2, 0)
+        weave_signalling(0, 2, "vector")
+        density_to_psum()
+        quantise("sig", 2, 1)
+        weave_signalling(1, 2, "vector", relayed=True)
+        quantise("sig", 0, 2)
+        quantise("sig", 1, 2)
         load_access(GQ - 1)
 
-        tiles = TILES
-        ahead = 7
-        quarters = [(g, c, t) for g, c in tiles for t in range(PACK)]
-        for c in range(CH):
+        for c in range(C // HALF):
             for q in range(RQ):
                 saturate(q, c)
-        weave_sig(2, 2, "gpsimd", 0)
+        weave_signalling(2, 2, "gpsimd", relayed=True)
         occupy(0, 0)
         occupy(1, 0)
         for q in range(2):
-            quantise_h(q, 0)
-            for quarter in quarters[:ahead]:
-                signal_pass(*quarter, q)
-        quantise_sig(2, 2)
-        weave_sig(0, 3, "gpsimd", 0)
+            quantise("h", q, 0)
+            for k in range(BANKS):
+                signal_pass(k, q)
+        quantise("sig", 2, 2)
+        weave_signalling(0, 3, "gpsimd", relayed=True)
         occupy(2, 0)
         occupy(0, 1)
-        quantise_h(2, 0)
-        for quarter in quarters[:ahead]:
-            signal_pass(*quarter, 2)
-        quantise_h(0, 1)
-        quantise_sig(0, 3)
-        weave_sig(1, 3, "gpsimd", 0)
+        quantise("h", 2, 0)
+        for k in range(BANKS):
+            signal_pass(k, 2)
+        quantise("sig", 0, 3)
+        weave_signalling(1, 3, "gpsimd", relayed=True)
         occupy(1, 1)
         occupy(2, 1)
+        weave_signalling(2, 3, "scalar")
 
-        def cast(i, part, on_scalar):
-            return lambda: round_y(*tiles[i], part, on_scalar)
-
-        def finish(i):
-            def run():
-                quantise_y(*tiles[i], 0, HALF)
-                if i == 4:
-                    store_scales(0, 2)
-                if i == 5:
-                    store_scales(2, 3)
-            return run
-
-        def job(fn, *args):
-            return lambda: fn(*args)
-
-        extras = {
-
-            (0, 3): [job(quantise_h, 1, 1), job(quantise_h, 2, 1)],
-            (2, 3): [cast(0, 0, True), cast(0, 1, True)],
-            (3, 1): [finish(0), cast(1, 0, True)],
-            (3, 3): [cast(1, 1, True), job(quantise_sig, 1, 3), job(weave_sig, 2, 3)],
-            (4, 1): [cast(2, 0, True), job(quantise_sig, 2, 3), finish(1)],
-            (4, 3): [cast(2, 1, True)],
-            (5, 1): [cast(3, 0, True), finish(2)],
-            (5, 3): [cast(3, 1, True), cast(4, 0, False), cast(4, 1, False), finish(3)],
-            (6, 1): [finish(4)],
-            (6, 3): [cast(5, 0, True), cast(5, 1, False)],
-            (7, 1): [cast(6, 0, False), finish(5)],
-            (7, 3): [cast(6, 1, True)],
-
+        last = len(TILES) - 1
+        after = {
+            3: [(quantise, "h", q, 1) for q in range(RQ)],
+            11: [(round_y, 0, 0, on_scalar), (quantise, "sig", 1, 3)],
+            13: [(round_y, 0, 1, on_scalar)],
+            14: [(round_y, 1, 0, on_vector)],
+            15: [(round_y, 1, 1, on_scalar)],
+            17: [(quantise, "sig", 2, 3)],
+            19: [(quantise_y, 0)],
+            20: [(round_y, 2, 0, on_scalar), (quantise_y, 1)],
+            23: [(round_y, 2, 1, on_scalar), (round_y, 3, 0, on_vector), (quantise_y, 2)],
+            25: [(round_y, 3, 1, on_scalar), (round_y, 4, 0, on_vector), (quantise_y, 3)],
+            29: [(round_y, 5, 0, on_scalar), (round_y, 4, 1, on_vector), (quantise_y, 4)],
+            31: [
+                (round_y, 6, 0, on_scalar),
+                (round_y, 5, 1, on_vector),
+                (quantise_y, 5),
+                (round_y, 7, 0, on_scalar),
+                (round_y, 6, 1, on_vector),
+                (round_y, 7, 1, on_scalar),
+                (quantise_y, 6),
+                (quantise_y, 7, 0, HALF // 2),
+                (quantise_y, 7, HALF // 2, HALF),
+                (store_scales,),
+            ],
         }
-        n = len(tiles)
-        for i, (g, c) in enumerate(tiles):
-            for t in range(PACK):
-                activate(g, c, t)
-                transcribe(g, c, t)
-                if t % 2 == 1:
-                    store_y(g, c, t - 1, t + 1)
-                for extra in extras.get((i, t), []):
-                    extra()
-                nxt = i * PACK + t + ahead
-                if nxt < n * PACK:
-                    for q in range(RQ):
-                        signal_pass(*tiles[nxt // PACK], nxt % PACK, q)
-        g, c = tiles[-1]
-        round_y(g, c, 0, False)
-        round_y(g, c, 1, True)
-        finish(n - 2)()
-        quantise_y(g, c, 0, HALF // 2)
-        quantise_y(g, c, HALF // 2, HALF)
-        store_scales(g, g + 1, last=True)
+        for k in range(len(QUARTERS)):
+            transcribe(k)
+            if k // PACK == last:
+                store_y(k, k)
+            elif k % 2 == 1:
+                store_y(k - 1, k)
+            for step in after.get(k, []):
+                step[0](*step[1:])
+            if k + BANKS < len(QUARTERS):
+                for q in range(RQ):
+                    signal_pass(k + BANKS, q)

from contextlib import ExitStack

import concourse.mybir as mybir
from concourse.masks import make_identity

R, L, C, G = 1536, 512, 1024, 2048
FLOPS = 2 * R * L * C + 2 * R * G * C

F32 = mybir.dt.float32
BF16 = mybir.dt.bfloat16
U32 = mybir.dt.uint32
I32 = mybir.dt.int32
U8 = mybir.dt.uint8
FP8X4 = mybir.dt.float8_e4m3fn_x4
ACT = mybir.ActivationFunctionType
MULT = mybir.AluOpType.mult
ADD = mybir.AluOpType.add

P = 128
PACK = 4
GROUP = P * PACK
HALF = 512
RQ = R // GROUP
GQ = G // GROUP
RUN = 4
TINY = 2.0**-60

DENSITY_ROW, BASAL_ROW, VMAX_ROW, VECTOR_ROWS = 0, 4, 8, 12

BANKS = 7

TILES = [(0, 0), (1, 0), (2, 0), (0, 1), (1, 1), (2, 1), (3, 0), (3, 1)]
QUARTERS = [(g, c, t) for g, c in TILES for t in range(PACK)]


def tile_receptor_occupancy_transcription_h3_kernel(
    tc, affinity, doses, density, signalling, basal, vmax, access, out_0, out_1, out_2
):
    nc = tc.nc
    with ExitStack() as ctx:
        keep = ctx.enter_context(tc.tile_pool(name="keep", bufs=1))
        stage = ctx.enter_context(tc.tile_pool(name="stage", bufs=8))
        loads = ctx.enter_context(tc.tile_pool(name="loads", bufs=9))
        wide = ctx.enter_context(tc.tile_pool(name="wide", bufs=7))
        y_words = ctx.enter_context(tc.tile_pool(name="y_words", bufs=3))
        psum = ctx.enter_context(tc.psum_pool(name="psum", bufs=BANKS))
        psum_vectors = ctx.enter_context(tc.psum_pool(name="psum_vectors", bufs=1))
        relay = ctx.enter_context(tc.tile_pool(name="relay", bufs=1))
        ctx.enter_context(tc.manual_schedule())

        live = {}

        def staged(key):
            live[key] = stage.tile([P, GROUP * PACK], BF16, name="staged", tag="stage", align_bytes=64)
            return live[key]

        def quantise(name, *index):
            label = "_".join([name] + [str(i) for i in index])
            codes = keep.tile([P, GROUP], U32, name="codes_" + label, align_bytes=64)
            scales = keep.tile([P, GROUP], U8, name="scales_" + label, align_bytes=64)
            live[(name,) + index] = (codes, scales)
            nc.vector.quantize_mx(
                out=codes[:].bitcast(FP8X4), scales=scales[:], in_=live[(name + "_in",) + index][:]
            )

        def multiply(out, stationary, columns, moving, wells, start, stop):
            nc.tensor.matmul_mx(
                out=out,
                lhsT=stationary[0][:, columns].bitcast(FP8X4),
                lhsT_scale=stationary[1][:, columns],
                rhs=moving[0][:, wells].bitcast(FP8X4),
                rhs_scale=moving[1][:, wells],
                start=start,
                stop=stop,
            )

        ident = keep.tile([P, P], F32, name="ident")
        tiny = keep.tile([P, 1], F32, name="tiny")
        one = keep.tile([P, 1], F32, name="one")
        zero = keep.tile([P, 1], F32, name="zero")
        y_scales = keep.tile([P, C], U8, name="y_scales", align_bytes=64)
        vector_rows = keep.tile([P, GROUP], BF16, name="rows")
        vectors = keep.tile([P, VECTOR_ROWS, PACK], BF16, name="vectors")
        density_wide = keep.tile([P, P], F32, name="density_wide")
        nc.gpsimd.memset(one[:], 1.0)
        nc.gpsimd.memset(tiny[:], TINY)
        make_identity(nc, ident[:])
        nc.gpsimd.memset(vector_rows[:].bitcast(I32), 0)
        nc.gpsimd.memset(density_wide[:], 0.0)
        nc.scalar.activation(out=zero[:], in_=one[:], func=ACT.Ln)


        def load_affinity(q, t0=0, t1=PACK):
            if t0 == 0:
                staged(("aff_raw", q))
            nc.sync.dma_start(
                out=live["aff_raw", q][:].rearrange("p (t k) -> p t k", t=PACK)[:, t0:t1, :],
                in_=affinity[q * GROUP : (q + 1) * GROUP, :].rearrange("(m t) k -> m t k", t=PACK)[:, t0:t1, :],
            )

        def load_doses(c):
            nc.sync.dma_start(
                out=staged(("dos_raw", c))[:].rearrange("p (j w) -> p j w", j=PACK),
                in_=doses[:, c * HALF : (c + 1) * HALF].rearrange("(p j) w -> p j w", j=PACK),
            )

        def load_signalling(q, pair):
            raw = loads.tile([P, PACK, 2 * GROUP], BF16, name="sig_raw", tag="loads")
            live["sig_raw", q, pair] = raw
            block = signalling[q * GROUP : (q + 1) * GROUP, pair * 2 * GROUP : (pair + 1) * 2 * GROUP]
            nc.sync.dma_start(out=raw[:], in_=block.rearrange("(p j) w -> p j w", j=PACK))

        def load_access(g):
            raw = loads.tile([P, PACK, C], BF16, name="access", tag="loads")
            live["access", g] = raw
            nc.sync.dma_start(
                out=raw[:], in_=access[g * GROUP : (g + 1) * GROUP, :].rearrange("(p t) w -> p t w", t=PACK)
            )

        def load_vectors():
            pieces = [
                (DENSITY_ROW, density, 0, 2),
                (DENSITY_ROW, density, 2, RQ),
                (BASAL_ROW, basal, 0, GQ),
                (VMAX_ROW, vmax, 0, GQ),
            ]
            for row, vector, q0, q1 in pieces:
                nc.sync.dma_start(
                    out=vector_rows[row + q0 : row + q1, :], in_=vector.rearrange("(q k) -> q k", k=GROUP)[q0:q1, :]
                )


        def turn_vectors():
            words = vector_rows[:].bitcast(F32)
            bank = psum_vectors.tile([P, 2, P], F32, name="vector_bank", tag="vector_bank")
            live["vector_bank"] = bank
            for u in range(2):
                nc.tensor.transpose(bank[:, u, :], words[:, u : GROUP // 2 : 2], ident[:])

        def empty_vectors():
            nc.vector.tensor_copy(
                out=vectors[:].rearrange("p r t -> p (r t)").bitcast(F32).rearrange("p (r u) -> p r u", u=2),
                in_=live["vector_bank"][:, :, 0:VECTOR_ROWS].rearrange("p u r -> p r u"),
            )

        def widen_density():
            nc.vector.tensor_copy(
                out=density_wide[:, 0 : RQ * PACK],
                in_=vectors[:, DENSITY_ROW : DENSITY_ROW + RQ, :].rearrange("p r t -> p (r t)"),
            )

        def density_to_psum():
            bank = psum_vectors.tile([P, P], F32, name="vector_bank", tag="vector_bank")
            nc.tensor.transpose(bank[:], density_wide[:], ident[:])
            turned = keep.tile([P, P], F32, name="density_turned")
            nc.vector.tensor_copy(out=turned[:], in_=bank[:])
            live["density"] = psum_vectors.tile([P, P], F32, name="vector_bank", tag="vector_bank")
            nc.tensor.transpose(live["density"][:], turned[:], ident[:])


        def turn_affinity(q, pair):
            words = live["aff_raw", q][:].bitcast(F32).rearrange("p (t w) -> p t w", t=PACK)
            bank = psum.tile([P, 2, 2, P], F32, name="bank", tag="bank")
            live["aff_bank", q, pair] = bank
            for t in range(2):
                for u in range(2):
                    nc.tensor.transpose(bank[:, t, u, :], words[:, 2 * pair + t, u : L // 2 : 2], ident[:])

        def empty_affinity(q, pair, copy):
            if pair == 0:
                staged(("aff_in", q))
            words = live["aff_in", q][:].bitcast(F32).rearrange("p (t m u) -> p t m u", t=PACK, u=2)
            copy(
                out=words[:, 2 * pair : 2 * pair + 2, :, :],
                in_=live["aff_bank", q, pair][:].rearrange("p t u m -> p t m u"),
            )

        def weave_doses(c):
            nc.vector.tensor_copy(
                out=staged(("dos_in", c))[:].rearrange("p (w i j) -> p w j i", i=RUN, j=PACK),
                in_=live["dos_raw", c][:].rearrange("p (j w i) -> p w j i", j=PACK, i=RUN),
            )

        def drive(q, c, b):
            bank = psum.tile([P, PACK, P], F32, name="bank", tag="bank")
            wells = slice(b * P, (b + 1) * P)
            for t in range(PACK):
                multiply(bank[:, t, :], live["aff", q], slice(t * P, (t + 1) * P), live["dos", c], wells, True, True)
            if b == 0:
                live["bound", q, c] = wide.tile([P, HALF, PACK], F32, name="bound", tag="wide")
            nc.scalar.activation(
                out=live["bound", q, c][:, wells, :], in_=bank[:].rearrange("p t w -> p w t"), func=ACT.Ln, bias=tiny[:]
            )

        def saturate(q, c):
            bound = live["bound", q, c]
            nc.scalar.activation(out=bound[:], in_=bound[:], func=ACT.Sigmoid, bias=zero[:])

        def occupy(q, c):
            nc.vector.tensor_tensor(
                out=staged(("h_in", q, c))[:].rearrange("p (w t) -> p w t", t=PACK),
                in0=live["bound", q, c][:],
                in1=live["density"][:, q * PACK : (q + 1) * PACK].unsqueeze(1).to_broadcast([P, HALF, PACK]),
                op=MULT,
            )


        def weave_signalling(q, g, engine, relayed=False):
            if relayed:
                live["sig_in", q, g] = relay.tile([P, GROUP * PACK], BF16, name="relay", tag="relay", align_bytes=64)
            else:
                staged(("sig_in", q, g))
            woven = live["sig_in", q, g][:].rearrange("p (t m j) -> p t m j", t=PACK, j=PACK)
            raw = live["sig_raw", q, g // 2][:, :, (g % 2) * GROUP : (g % 2 + 1) * GROUP]
            raw = raw.rearrange("p j (m t) -> p t m j", t=PACK)
            if engine == "gpsimd":
                nc.gpsimd.tensor_scalar(out=woven, in0=raw, scalar1=1.0, scalar2=0.0, op0=MULT, op1=ADD)
            else:
                copy = nc.vector.tensor_copy if engine == "vector" else nc.scalar.copy
                copy(out=woven.rearrange("p t m j -> p m j t"), in_=raw.rearrange("p t m j -> p m j t"))

        def signal_pass(k, q):
            g, c, t = QUARTERS[k]
            if q == 0:
                live["z", k] = psum.tile([P, HALF], F32, name="bank", tag="bank")
            columns = slice(t * P, (t + 1) * P)
            multiply(live["z", k][:], live["sig", q, g], columns, live["h", q, c], slice(0, HALF), q == 0, q == RQ - 1)

        def transcribe(k):
            g, c, t = QUARTERS[k]
            if t == 0:
                live["y", g, c] = wide.tile([P, PACK, HALF], F32, name="y", tag="wide")
            y = live["y", g, c][:, t, :]
            nc.scalar.activation(
                out=y, in_=live["z", k][:], func=ACT.Sigmoid, bias=vectors[:, BASAL_ROW + g, t : t + 1]
            )
            nc.vector.scalar_tensor_tensor(
                out=y,
                in0=y,
                scalar=vectors[:, VMAX_ROW + g, t : t + 1],
                in1=live["access", g][:, t, c * HALF : (c + 1) * HALF],
                op0=MULT,
                op1=MULT,
            )

        def store_y(k0, k1):
            g, c, t0 = QUARTERS[k0]
            values = slice(t0, QUARTERS[k1][2] + 1)
            rows = out_0[g * GROUP : (g + 1) * GROUP, c * HALF : (c + 1) * HALF].rearrange("(p t) w -> p t w", t=PACK)
            nc.sync.dma_start(out=rows[:, values, :], in_=live["y", g, c][:, values, :])

        def round_y(i, part, copy):
            g, c = TILES[i]
            if part == 0:
                staged(("y_in", i))
            w0, w1 = part * HALF // 2, (part + 1) * HALF // 2
            copy(
                out=live["y_in", i][:, w0 * PACK : w1 * PACK].rearrange("p (w i t) -> p w t i", i=RUN, t=PACK),
                in_=live["y", g, c][:, :, w0:w1].rearrange("p t (w i) -> p w t i", i=RUN),
            )

        def quantise_y(i, w0=0, w1=HALF):
            g, c = TILES[i]
            if w0 == 0:
                live["y_codes", i] = y_words.tile([P, HALF], U32, name="y_codes", tag="y_words", align_bytes=64)
            codes = live["y_codes", i][:, w0:w1]
            wells = slice(c * HALF + w0, c * HALF + w1)
            nc.vector.quantize_mx(
                out=codes.bitcast(FP8X4),
                scales=y_scales[4 * g : P, wells],
                in_=live["y_in", i][:, w0 * PACK : w1 * PACK],
            )
            words = out_1[g].rearrange("p w t -> p (w t)").bitcast(I32)
            nc.sync.dma_start(out=words[:, wells], in_=codes.bitcast(I32))

        def store_scales():
            for quad in range(4):
                queue = nc.scalar if quad % 2 == 1 else nc.sync
                queue.dma_start(
                    out=out_2[:, 4 * quad : 4 * quad + 4, :].bitcast(I32),
                    in_=y_scales[32 * quad : 32 * quad + 4 * GQ, :].bitcast(I32),
                )

        on_scalar, on_vector = nc.scalar.copy, nc.vector.tensor_copy

        load_doses(0)
        load_affinity(0, 0, 2)
        load_affinity(0, 2, PACK)
        load_affinity(1)
        load_affinity(2)
        load_signalling(0, 0)
        load_doses(1)
        load_signalling(1, 0)
        load_signalling(2, 0)
        load_vectors()
        for q in range(RQ):
            load_signalling(q, 1)
        for g in range(GQ - 1):
            load_access(g)

        weave_doses(0)
        turn_affinity(0, 0)
        empty_affinity(0, 0, on_scalar)
        turn_affinity(0, 1)
        quantise("dos", 0)
        empty_affinity(0, 1, on_vector)
        quantise("aff", 0)
        turn_affinity(1, 0)
        empty_affinity(1, 0, on_scalar)
        turn_affinity(1, 1)
        empty_affinity(1, 1, on_vector)
        drive(0, 0, 0)
        drive(0, 0, 1)
        quantise("aff", 1)
        drive(0, 0, 2)
        drive(0, 0, 3)
        weave_signalling(0, 0, "vector")
        for pair in range(2):
            turn_affinity(2, pair)
            empty_affinity(2, pair, on_scalar)
        weave_doses(1)
        quantise("aff", 2)
        quantise("dos", 1)
        weave_signalling(0, 1, "vector")
        quantise("sig", 0, 0)
        for q, c in [(1, 0), (2, 0), (0, 1)]:
            for b in range(HALF // P):
                drive(q, c, b)
        turn_vectors()
        for q, c in [(1, 1), (2, 1)]:
            for b in range(HALF // P):
                drive(q, c, b)

        weave_signalling(1, 0, "vector")
        quantise("sig", 0, 1)
        weave_signalling(1, 1, "vector")
        quantise("sig", 1, 0)
        weave_signalling(2, 0, "vector")
        quantise("sig", 1, 1)
        empty_vectors()
        weave_signalling(2, 1, "vector")
        widen_density()
        quantise("sig", 2, 0)
        weave_signalling(0, 2, "vector")
        density_to_psum()
        quantise("sig", 2, 1)
        weave_signalling(1, 2, "vector", relayed=True)
        quantise("sig", 0, 2)
        quantise("sig", 1, 2)
        load_access(GQ - 1)

        for c in range(C // HALF):
            for q in range(RQ):
                saturate(q, c)
        weave_signalling(2, 2, "gpsimd", relayed=True)
        occupy(0, 0)
        occupy(1, 0)
        for q in range(2):
            quantise("h", q, 0)
            for k in range(BANKS):
                signal_pass(k, q)
        quantise("sig", 2, 2)
        weave_signalling(0, 3, "gpsimd", relayed=True)
        occupy(2, 0)
        occupy(0, 1)
        quantise("h", 2, 0)
        for k in range(BANKS):
            signal_pass(k, 2)
        quantise("sig", 0, 3)
        weave_signalling(1, 3, "gpsimd", relayed=True)
        occupy(1, 1)
        occupy(2, 1)
        weave_signalling(2, 3, "scalar")

        last = len(TILES) - 1
        after = {
            3: [(quantise, "h", q, 1) for q in range(RQ)],
            11: [(round_y, 0, 0, on_scalar), (quantise, "sig", 1, 3)],
            13: [(round_y, 0, 1, on_scalar)],
            14: [(round_y, 1, 0, on_vector)],
            15: [(round_y, 1, 1, on_scalar)],
            17: [(quantise, "sig", 2, 3)],
            19: [(quantise_y, 0)],
            20: [(round_y, 2, 0, on_scalar), (quantise_y, 1)],
            23: [(round_y, 2, 1, on_scalar), (round_y, 3, 0, on_vector), (quantise_y, 2)],
            25: [(round_y, 3, 1, on_scalar), (round_y, 4, 0, on_vector), (quantise_y, 3)],
            29: [(round_y, 5, 0, on_scalar), (round_y, 4, 1, on_vector), (quantise_y, 4)],
            31: [
                (round_y, 6, 0, on_scalar),
                (round_y, 5, 1, on_vector),
                (quantise_y, 5),
                (round_y, 7, 0, on_scalar),
                (round_y, 6, 1, on_vector),
                (round_y, 7, 1, on_scalar),
                (quantise_y, 6),
                (quantise_y, 7, 0, HALF // 2),
                (quantise_y, 7, HALF // 2, HALF),
                (store_scales,),
            ],
        }
        for k in range(len(QUARTERS)):
            transcribe(k)
            if k // PACK == last:
                store_y(k, k)
            elif k % 2 == 1:
                store_y(k - 1, k)
            for step in after.get(k, []):
                step[0](*step[1:])
            if k + BANKS < len(QUARTERS):
                for q in range(RQ):
                    signal_pass(k + BANKS, q)
